import numpy as np
import ml_dtypes


def mxq(x, axis, fmt="e4m3"):
    dtype, down = {"e4m3": (ml_dtypes.float8_e4m3fn, 7), "e5m2": (ml_dtypes.float8_e5m2, 14)}[fmt]
    v = np.moveaxis(np.asarray(x, np.float32).astype(ml_dtypes.bfloat16).astype(np.float64), axis, -1)
    blocks = v.reshape(v.shape[:-1] + (-1, 32))
    amax = np.abs(blocks).max(-1, keepdims=True)
    byte = np.maximum(np.where(amax > 0, np.frexp(amax)[1] - 1 + 127, 0) - down, 1)
    scale = np.exp2(byte - 127.0)
    codes = (blocks / scale).astype(np.float32).astype(dtype).astype(np.float64)
    return np.moveaxis((codes * scale).reshape(v.shape), -1, axis)


WIDE = False


def mx_kscale(k):
    if not WIDE:
        return np.ones(k)
    levels = np.array([10, -10, 5, -5, 0])
    if k % 512:
        return np.exp2(np.random.permutation(np.resize(levels, k // 32))).repeat(32)
    a = np.empty((k // 512, 16))
    for p in range(k // 512):
        a[p, :8] = np.random.permutation(np.resize(levels, 8))
        for g in range(8):
            far = levels[np.abs(levels - a[p, g]) >= 10]
            a[p, g + 8] = far[np.random.randint(len(far))]
    return np.exp2(a.ravel()).repeat(32)


def f64(x):
    return np.asarray(x).astype(np.float64)


def striped(idx):
    return np.tile(idx.reshape(-1, 16).T, (8, 1)).astype(np.uint16)


def unstriped(offs):
    return offs[:16].T.reshape(-1).astype(np.int64)


E2M1 = np.array([0.0, 0.5, 1.0, 1.5, 2.0, 3.0, 4.0, 6.0, -0.0, -0.5, -1.0, -1.5, -2.0, -3.0, -4.0, -6.0])


def pack_weight(w, fmt):
    k, n = w.shape
    w = f64(np.asarray(w, np.float32).astype(ml_dtypes.bfloat16)).reshape(k // 32, 32, n)
    amax = np.abs(w).max(1)
    if fmt == "e4m3":
        byte = np.frexp(amax)[1] - 1 + 127 - 7
    else:
        mant, ex = np.frexp(amax / 6.0)
        byte = np.where(mant > 0.5, ex, ex - 1) + 127
    byte = np.clip(np.where(amax > 0, byte, 1), 1, 254)
    scaled = (w * np.exp2(127.0 - byte)[:, None, :]).reshape(k, n).astype(np.float32)
    by_word = np.ascontiguousarray(scaled.reshape(k // 512, 128, 4, n).transpose(0, 1, 3, 2))
    if fmt == "e4m3":
        words = by_word.astype(ml_dtypes.float8_e4m3fn).view(np.uint8)
    else:
        c = by_word.astype(ml_dtypes.float4_e2m1fn).view(np.uint8) & 0xF
        words = (c[..., 0::2] | (c[..., 1::2] << 4)).reshape(k // 512, 128, 2 * n)
    return np.ascontiguousarray(words), np.ascontiguousarray(byte.astype(np.uint8).reshape(k // 512, 16, n))


def unpack_weight(words, scales, fmt):
    g, _, n = scales.shape
    words = np.ascontiguousarray(words).reshape(g, 128, n, -1)
    if fmt == "e4m3":
        vals = words.view(ml_dtypes.float8_e4m3fn).astype(np.float64)
    else:
        nib = np.empty((g, 128, n, 4), np.uint8)
        nib[..., 0::2] = words & 0xF
        nib[..., 1::2] = words >> 4
        vals = E2M1[nib]
    vals = vals * np.repeat(np.exp2(scales.astype(np.float64) - 127.0), 8, axis=1)[..., None]
    return vals.transpose(0, 1, 3, 2).reshape(g * 512, n)


def gelu(v):
    return 0.5 * v * (1.0 + np.tanh(np.sqrt(2.0 / np.pi) * (v + 0.044715 * v**3)))


K, KA, KB, H, T, S, S2, T3 = 2048, 1024, 1024, 1024, 2048, 512, 512, 2048

def setup_inputs():
    n = np.random.standard_normal
    s = mx_kscale(K)[:, None]
    u = mx_kscale(H)[:, None]
    tab_words, tab_scales = pack_weight(n((K, T)) * s, "e4m3")
    tab2_words, tab2_scales = pack_weight(0.7 * n((H, T3)) / np.sqrt(H) / u, "e4m3")
    tab3_words, tab3_scales = pack_weight(n((H, T3)) / np.sqrt(H) / u, "e4m3")
    w4_words, w4_scales = pack_weight(1.1 * n((KA, H)) / np.sqrt(K) / s[:KA], "e2m1")
    return {
        "tab_words": tab_words, "tab_scales": tab_scales,
        "tab2_words": tab2_words, "tab2_scales": tab2_scales,
        "tab3_words": tab3_words, "tab3_scales": tab3_scales,
        "w4_words": w4_words, "w4_scales": w4_scales,
        "w1": (1.1 * n((KB, H)) / np.sqrt(K) / s[KA:]).astype(np.float32),
        "b1": (0.5 * n(H)).astype(np.float32),
        "gain": (np.exp(0.3 * n(H)) * u[:, 0]).astype(np.float32),
        "res": (0.7 * n((H, S)) * u).astype(np.float32),
        "c2": (0.5 * n(S2)).astype(np.float32),
        "offs": striped(np.random.permutation(T)[:S]),
        "offs2": striped(np.random.permutation(T3)[:S2]),
        "offs3": striped(np.random.permutation(T3)[:S2]),
    }

def reference(tab_words, tab_scales, tab2_words, tab2_scales, tab3_words, tab3_scales,
              w4_words, w4_scales, w1, b1, gain, res, c2, offs, offs2, offs3):
    v = unpack_weight(tab_words, tab_scales, "e4m3")[:, unstriped(offs)]
    v2 = unpack_weight(tab2_words, tab2_scales, "e4m3")[:, unstriped(offs2)]
    v3 = unpack_weight(tab3_words, tab3_scales, "e4m3")[:, unstriped(offs3)]
    w4 = unpack_weight(w4_words, w4_scales, "e2m1")
    w1q = mxq(f64(w1), 0, "e4m3")
    y = w4.T @ v[:KA] + w1q.T @ v[KA:]
    h = f64(gain)[:, None] * np.tanh(y + f64(b1)[:, None])
    hr = h + f64(res)
    e2 = v2.T @ mxq(h, 0, "e4m3")
    e3 = v3.T @ mxq(hr, 0, "e4m3")
    return np.sin(e2) * e3 + f64(c2)[:, None]

@@ -1,0 +1,277 @@
+import math
+from contextlib import ExitStack
+
+import concourse.mybir as mybir
+
+K, KA, KB, H, T, S, S2 = 2048, 1024, 1024, 1024, 2048, 512, 512
+FLOPS = 2 * (K * H * S + 2 * H * S2 * S)
+
+F32 = mybir.dt.float32
+BF16 = mybir.dt.bfloat16
+I32 = mybir.dt.int32
+U32 = mybir.dt.uint32
+U16 = mybir.dt.uint16
+U8 = mybir.dt.uint8
+FP8X4 = mybir.dt.float8_e4m3fn_x4
+FP4X4 = mybir.dt.float4_e2m1fn_x4
+ACT = mybir.ActivationFunctionType
+ALU = mybir.AluOpType
+
+P = 128
+PACK = 4
+PASS = P * PACK
+QUADS = 4
+HALF = S // 2
+LOADS = 3
+
+
+def tile_list_companion_introduction_score_kernel(
+    tc, tab_words, tab_scales, tab2_words, tab2_scales, tab3_words, tab3_scales,
+    w4_words, w4_scales, w1, b1, gain, res, c2, offs, offs2, offs3, out,
+):
+    nc = tc.nc
+    with ExitStack() as ctx:
+        keep = ctx.enter_context(tc.tile_pool(name="keep", bufs=1))
+        psum = ctx.enter_context(tc.psum_pool(name="psum", bufs=1))
+
+        def held(shape, dtype, name):
+            return keep.tile(shape, dtype, name=name, align_bytes=64)
+
+        def ring(shape, dtype, tag, bufs):
+            return keep.tile(shape, dtype, name=tag, tag=tag, bufs=bufs, align_bytes=64)
+
+        def bank(n):
+            return psum.tile([P, S], F32, name="bank%d" % n, tag="bank%d" % n)
+
+        def load_list(src, name):
+            tile = keep.tile([P, S // 16], U16, name=name)
+            nc.sync.dma_start(tile[:], src)
+            return tile
+
+        def load_words(words, a):
+            tile = ring([P, T], U32, "load", LOADS)
+            nc.sync.dma_start(out=tile[:].bitcast(I32), in_=words[a].rearrange("p t i -> p (t i)").bitcast(I32))
+            return tile
+
+        def load_rows(rows):
+            tile = ring([P, PACK, rows.shape[1]], F32, "load", LOADS)
+            nc.sync.dma_start(out=tile[:], in_=rows.rearrange("(p i) c -> p i c", i=PACK))
+            return tile
+
+        def gather(window, offsets, dtype, name):
+            tile = held([P, S], dtype, name)
+            nc.vector.tensor_copy(tile[:], window.indirect(offsets[:]))
+            return tile
+
+        def quantise(values, codes, scales):
+            nc.vector.quantize_mx(out=codes.bitcast(FP8X4), scales=scales, in_=values)
+
+        def by_lines_in(planes):
+            return planes.rearrange("p i (c e) -> p c i e", e=4)
+
+        def by_lines_out(woven):
+            return woven.rearrange("p (c e i) -> p c i e", e=4, i=PACK)
+
+        tab_sc = held([P, 2, T], U8, "tab_sc")
+        w4_sc = held([P, 2, H], U8, "w4_sc")
+        tab2_sc = held([P, T], U8, "tab2_sc")
+        tab3_sc = held([P, T], U8, "tab3_sc")
+        for tile in (tab_sc, w4_sc, tab2_sc, tab3_sc):
+            nc.vector.memset(tile[:].bitcast(I32), 0)
+        phase = keep.tile([P, 1], F32, name="phase")
+        one = keep.tile([P, 1], F32, name="one")
+        nc.vector.memset(one[:], 1.0)
+        nc.vector.tensor_scalar(phase[:], one[:], -math.pi / 8, None, ALU.mult)
+
+        def load_scale_rows(queue, tile_rows, rows):
+            queue.dma_start(out=tile_rows.bitcast(I32), in_=rows.bitcast(I32))
+
+        w_rows = {}
+        w_rows[0, 0] = load_rows(w1[0:PASS, 0:PASS])
+        idx = load_list(offs, "idx")
+        w_rows[0, 1] = load_rows(w1[PASS : 2 * PASS, 0:PASS])
+        w4_raw = held([P, 2, H], U16, "w4_raw")
+        nc.sync.dma_start(out=w4_raw[:].bitcast(I32), in_=w4_words.rearrange("a p c -> p a c").bitcast(I32))
+        tab_win = {2: load_words(tab_words, 2)}
+        idx2 = load_list(offs2, "idx2")
+        idx3 = load_list(offs3, "idx3")
+        for upper in (1, 0):
+            for q in range(QUADS):
+                first = 32 * q + 4 * upper
+                load_scale_rows(nc.sync, tab_sc[first : first + 4, :, :],
+                                tab_scales[2 * upper : 2 * upper + 2, 4 * q : 4 * q + 4, :].rearrange("a r t -> r a t"))
+        for q in range(QUADS):
+            load_scale_rows(nc.sync, w4_sc[32 * q : 32 * q + 4, :, :], w4_scales[:, 4 * q : 4 * q + 4, :].rearrange("a r c -> r a c"))
+
+        b1_sb = keep.tile([P, 2, PACK], F32, name="b1_sb")
+        gain_sb = keep.tile([P, 2, PACK], F32, name="gain_sb")
+        c2_sb = keep.tile([P, QUADS], F32, name="c2_sb")
+        nc.gpsimd.dma_start(out=b1_sb[:], in_=b1.rearrange("(b p i) -> p b i", p=P, i=PACK))
+        nc.gpsimd.dma_start(out=gain_sb[:], in_=gain.rearrange("(b p i) -> p b i", p=P, i=PACK))
+        for tile, scales in ((tab2_sc, tab2_scales), (tab3_sc, tab3_scales)):
+            for q in range(QUADS):
+                load_scale_rows(nc.gpsimd, tile[32 * q + 8 : 32 * q + 16, :], scales[:, 4 * q : 4 * q + 4, :])
+        with nc.allow_non_contiguous_dma(reason="one value of c2 for each partition and output tile"):
+            nc.gpsimd.dma_start(out=c2_sb[:], in_=c2.rearrange("(m p) -> p m", p=P))
+
+        for a in (3, 0, 1):
+            tab_win[a] = load_words(tab_words, a)
+        w_rows[1, 0] = load_rows(w1[0:PASS, PASS : 2 * PASS])
+        w_rows[1, 1] = load_rows(w1[PASS : 2 * PASS, PASS : 2 * PASS])
+        tab2_win = [load_words(tab2_words, a) for a in range(2)]
+        res0 = load_rows(res[0:PASS, :])
+        tab3_win = [load_words(tab3_words, a) for a in range(2)]
+        res1 = [load_rows(res[PASS : 2 * PASS, jh * HALF : (jh + 1) * HALF]) for jh in range(2)]
+
+        w1_codes, w1_scales = {}, {}
+
+        def round_w1(engine_copy, b, a):
+            woven = ring([P, PACK * PASS], BF16, "w1_bf", 2)
+            engine_copy(
+                out=woven[:].rearrange("p (t m j) -> p m j t", t=PACK, j=PACK),
+                in_=w_rows[b, a][:].rearrange("p j (m t) -> p m j t", t=PACK),
+            )
+            return woven
+
+        def quantise_w1(woven, b, a):
+            w1_codes[b, a] = held([P, PASS], U32, "w1_codes%d%d" % (b, a))
+            w1_scales[b, a] = held([P, PASS], U8, "w1_scales%d%d" % (b, a))
+            quantise(woven[:], w1_codes[b, a][:], w1_scales[b, a][:])
+
+        for a in range(2):
+            quantise_w1(round_w1(nc.scalar.copy, 0, a), 0, a)
+
+        w4_dealt = held([P, 2, H], U16, "w4_dealt")
+        nc.scalar.copy(
+            out=w4_dealt[:].rearrange("p a (b t m) -> p (a b) m t", b=2, t=PACK),
+            in_=w4_raw[:].rearrange("p a (b m t) -> p (a b) m t", b=2, t=PACK),
+        )
+
+        v_scales = [gather(tab_sc[:, s, :], idx, U8, "v_scales%d" % s) for s in range(2)]
+        v_codes = {}
+        for a in (2, 3):
+            v_codes[a] = gather(tab_win[a][:], idx, U32, "v_codes%d" % a)
+        w4_sc_dealt = held([P, 2, H], U8, "w4_sc_dealt")
+        nc.vector.tensor_copy(
+            out=w4_sc_dealt[:].rearrange("p a (b t m) -> p (a b) m t", b=2, t=PACK),
+            in_=w4_sc[:].rearrange("p a (b m t) -> p (a b) m t", b=2, t=PACK),
+        )
+        for a in (0, 1):
+            v_codes[a] = gather(tab_win[a][:], idx, U32, "v_codes%d" % a)
+
+        def first_stage_pass(acc, b, a, start, stop):
+            for i in range(PACK):
+                if a < 2:
+                    cols = slice(PASS * b + P * i, PASS * b + P * (i + 1))
+                    lhsT, lhsT_scale = w4_dealt[:, a, cols].bitcast(FP4X4), w4_sc_dealt[:, a, cols]
+                else:
+                    cols = slice(P * i, P * (i + 1))
+                    lhsT, lhsT_scale = w1_codes[b, a - 2][:, cols].bitcast(FP8X4), w1_scales[b, a - 2][:, cols]
+                nc.tensor.matmul_mx(
+                    out=acc[i][:], lhsT=lhsT, lhsT_scale=lhsT_scale,
+                    rhs=v_codes[a][:].bitcast(FP8X4), rhs_scale=v_scales[a % 2][4 * (a // 2) : P, :],
+                    start=start, stop=stop,
+                )
+
+        y = [[bank(PACK * b + i) for i in range(PACK)] for b in range(2)]
+        for n, a in enumerate((2, 3, 0, 1)):
+            first_stage_pass(y[0], 0, a, n == 0, n == 3)
+        for a in (0, 1):
+            first_stage_pass(y[1], 1, a, a == 0, False)
+
+        def first_result(b):
+            h = held([P, PACK, S], F32, "h%d" % b)
+            for i in range(PACK):
+                t = ring([P, S], F32, "tanh", 3)
+                nc.scalar.activation(out=t[:], in_=y[b][i][:], func=ACT.Tanh, bias=b1_sb[:, b, i : i + 1])
+                nc.scalar.activation(out=h[:, i, :], in_=t[:], func=ACT.Copy, scale=gain_sb[:, b, i : i + 1])
+            return h
+
+        h0 = first_result(0)
+        for a in range(2):
+            quantise_w1(round_w1(nc.vector.tensor_copy, 1, a), 1, a)
+            first_stage_pass(y[1], 1, 2 + a, False, a == 1)
+        h1 = first_result(1)
+
+        h_codes = [held([P, S], U32, "h_codes%d" % b) for b in range(2)]
+        h_scales = [held([P, S], U8, "h_scales%d" % b) for b in range(2)]
+        hr_codes0, hr_scales0 = held([P, S], U32, "hr_codes0"), held([P, S], U8, "hr_scales0")
+        hr_codes1 = [held([P, HALF], U32, "hr_codes1%d" % jh) for jh in range(2)]
+        hr_scales1 = [held([P, HALF], U8, "hr_scales1%d" % jh) for jh in range(2)]
+
+        def weave_h(h):
+            woven = ring([P, PACK * S], BF16, "woven", 3)
+            nc.vector.tensor_copy(out=by_lines_out(woven[:]), in_=by_lines_in(h[:]))
+            return woven[:]
+
+        def weave_hr(h_planes, res_planes):
+            width = h_planes.shape[2]
+            woven = ring([P, PACK * width], BF16, "woven", 3)
+            nc.vector.tensor_tensor(by_lines_out(woven[:]), by_lines_in(h_planes), by_lines_in(res_planes), ALU.add)
+            return woven[:]
+
+        v2_scales = gather(tab2_sc[:], idx2, U8, "v2_scales")
+        woven = weave_h(h0)
+        v2_codes = [gather(tab2_win[0][:], idx2, U32, "v2_codes0")]
+        quantise(woven, h_codes[0][:], h_scales[0][:])
+        v2_codes.append(gather(tab2_win[1][:], idx2, U32, "v2_codes1"))
+        woven = weave_h(h1)
+        v3_scales = gather(tab3_sc[:], idx3, U8, "v3_scales")
+        quantise(woven, h_codes[1][:], h_scales[1][:])
+
+        e2 = [bank(m) for m in range(QUADS)]
+        for b in range(2):
+            for m in range(QUADS):
+                cols = slice(P * m, P * (m + 1))
+                nc.tensor.matmul_mx(
+                    out=e2[m][:], lhsT=v2_codes[b][:, cols].bitcast(FP8X4), lhsT_scale=v2_scales[8 + 4 * b : P, cols],
+                    rhs=h_codes[b][:].bitcast(FP8X4), rhs_scale=h_scales[b][:], start=b == 0, stop=b == 1,
+                )
+
+        u = held([P, QUADS, S], F32, "u")
+        for m in range(QUADS):
+            a = ring([P, S], F32, "angle", 2)
+            nc.scalar.activation(out=a[:], in_=e2[m][:], func=ACT.Sin, bias=phase[:], scale=0.25)
+            nc.scalar.activation(out=a[:], in_=a[:], func=ACT.Square)
+            nc.scalar.activation(out=u[:, m, :], in_=a[:], func=ACT.Square, bias=one[:], scale=-2.0)
+
+        woven = weave_hr(h0[:], res0[:])
+        v3_codes = [gather(tab3_win[0][:], idx3, U32, "v3_codes0")]
+        quantise(woven, hr_codes0[:], hr_scales0[:])
+        v3_codes.append(gather(tab3_win[1][:], idx3, U32, "v3_codes1"))
+
+        e3 = {(jh, pair): bank(QUADS + 2 * jh + pair) for jh in range(2) for pair in range(2)}
+
+        def second_pass(jh, b, codes, scales):
+            for m in range(QUADS):
+                cols = slice(P * m, P * (m + 1))
+                nc.tensor.matmul_mx(
+                    out=e3[jh, m // 2][:, HALF * (m % 2) : HALF * (m % 2 + 1)],
+                    lhsT=v3_codes[b][:, cols].bitcast(FP8X4), lhsT_scale=v3_scales[8 + 4 * b : P, cols],
+                    rhs=codes.bitcast(FP8X4), rhs_scale=scales,
+                    start=b == 0 and m % 2 == 0, stop=b == 1 and m % 2 == 1,
+                )
+
+        for jh in range(2):
+            members = slice(HALF * jh, HALF * (jh + 1))
+            second_pass(jh, 0, hr_codes0[:, members], hr_scales0[:, members])
+        for jh in range(2):
+            members = slice(HALF * jh, HALF * (jh + 1))
+            woven = weave_hr(h1[:, :, members], res1[jh][:])
+            quantise(woven, hr_codes1[jh][:], hr_scales1[jh][:])
+            second_pass(jh, 1, hr_codes1[jh][:], hr_scales1[jh][:])
+        for jh in range(2):
+            members = slice(HALF * jh, HALF * (jh + 1))
+            for pair in range(2):
+                o = ring([P, 2, HALF], F32, "score", 4)
+                nc.vector.scalar_tensor_tensor(
+                    out=o[:], in0=u[:, 2 * pair : 2 * pair + 2, members], scalar=0.5,
+                    in1=e3[jh, pair][:].rearrange("p (m j) -> p m j", m=2), op0=ALU.subtract, op1=ALU.mult,
+                )
+                for m in range(2):
+                    nc.scalar.activation(
+                        out=o[:, m, :], in_=o[:, m, :], func=ACT.Identity,
+                        bias=c2_sb[:, 2 * pair + m : 2 * pair + m + 1], scale=2.0,
+                    )
+                rows = slice(2 * P * pair, 2 * P * (pair + 1))
+                nc.sync.dma_start(out=out[rows, members].rearrange("(m p) j -> p m j", p=P), in_=o[:])

@@ -22,7 +22,6 @@ PACK = 4
 PASS = P * PACK
 QUADS = 4
 HALF = S // 2
-LOADS = 3
 
 
 def tile_list_companion_introduction_score_kernel(
@@ -48,18 +47,18 @@ def tile_list_companion_introduction_score_kernel(
             nc.sync.dma_start(tile[:], src)
             return tile
 
-        def load_words(words, a):
-            tile = ring([P, T], U32, "load", LOADS)
+        def load_words(words, a, slot):
+            tile = ring([P, T], U32, slot, 1)
             nc.sync.dma_start(out=tile[:].bitcast(I32), in_=words[a].rearrange("p t i -> p (t i)").bitcast(I32))
             return tile
 
-        def load_rows(rows):
-            tile = ring([P, PACK, rows.shape[1]], F32, "load", LOADS)
+        def load_rows(rows, slot):
+            tile = ring([P, PACK, rows.shape[1]], F32, slot, 1)
             nc.sync.dma_start(out=tile[:], in_=rows.rearrange("(p i) c -> p i c", i=PACK))
             return tile
 
         def gather(window, offsets, dtype, name):
-            tile = held([P, S], dtype, name)
+            tile = ring([P, S], dtype, name, 1)
             nc.vector.tensor_copy(tile[:], window.indirect(offsets[:]))
             return tile
 
@@ -72,56 +71,48 @@ def tile_list_companion_introduction_score_kernel(
         def by_lines_out(woven):
             return woven.rearrange("p (c e i) -> p c i e", e=4, i=PACK)
 
-        tab_sc = held([P, 2, T], U8, "tab_sc")
-        w4_sc = held([P, 2, H], U8, "w4_sc")
-        tab2_sc = held([P, T], U8, "tab2_sc")
-        tab3_sc = held([P, T], U8, "tab3_sc")
-        for tile in (tab_sc, w4_sc, tab2_sc, tab3_sc):
-            nc.vector.memset(tile[:].bitcast(I32), 0)
-        phase = keep.tile([P, 1], F32, name="phase")
-        one = keep.tile([P, 1], F32, name="one")
-        nc.vector.memset(one[:], 1.0)
-        nc.vector.tensor_scalar(phase[:], one[:], -math.pi / 8, None, ALU.mult)
-
         def load_scale_rows(queue, tile_rows, rows):
             queue.dma_start(out=tile_rows.bitcast(I32), in_=rows.bitcast(I32))
 
-        w_rows = {}
-        w_rows[0, 0] = load_rows(w1[0:PASS, 0:PASS])
+        tab_sc = held([P, T], U8, "tab_sc")
+        w4_sc = held([P, 2, H], U8, "w4_sc")
+        tab2_sc = held([P, T], U8, "tab2_sc")
+        tab3_sc = held([P, T], U8, "tab3_sc")
+        for tile in (w4_sc, tab_sc):
+            nc.vector.memset(tile[:].bitcast(I32), 0)
+        seed = ring([P, 1], F32, "seed_then_b1", 1)
+        nc.vector.memset(seed[:], 1.0)
+        phase = keep.tile([P, 1], F32, name="phase")
+        nc.vector.tensor_scalar(phase[:], seed[:], -math.pi / 8, None, ALU.mult)
+        for tile in (tab3_sc, tab2_sc):
+            nc.vector.memset(tile[:].bitcast(I32), 0)
+
         idx = load_list(offs, "idx")
-        w_rows[0, 1] = load_rows(w1[PASS : 2 * PASS, 0:PASS])
-        w4_raw = held([P, 2, H], U16, "w4_raw")
-        nc.sync.dma_start(out=w4_raw[:].bitcast(I32), in_=w4_words.rearrange("a p c -> p a c").bitcast(I32))
-        tab_win = {2: load_words(tab_words, 2)}
-        idx2 = load_list(offs2, "idx2")
-        idx3 = load_list(offs3, "idx3")
-        for upper in (1, 0):
-            for q in range(QUADS):
-                first = 32 * q + 4 * upper
-                load_scale_rows(nc.sync, tab_sc[first : first + 4, :, :],
-                                tab_scales[2 * upper : 2 * upper + 2, 4 * q : 4 * q + 4, :].rearrange("a r t -> r a t"))
+        tab_win = {2: load_words(tab_words, 2, "tab_win2")}
+        b1_sb = ring([P, 2, PACK], F32, "seed_then_b1", 1)
+        nc.sync.dma_start(out=b1_sb[:], in_=b1.rearrange("(b p i) -> p b i", p=P, i=PACK))
         for q in range(QUADS):
             load_scale_rows(nc.sync, w4_sc[32 * q : 32 * q + 4, :, :], w4_scales[:, 4 * q : 4 * q + 4, :].rearrange("a r c -> r a c"))
+        w_rows = {}
+        w_rows[0, 0] = load_rows(w1[0:PASS, 0:PASS], "w1_then_res")
+        w4_raw = ring([P, 2, H], U16, "w4_then_tab", 1)
+        nc.sync.dma_start(out=w4_raw[:].bitcast(I32), in_=w4_words.rearrange("a p c -> p a c").bitcast(I32))
+        for q in range(QUADS):
+            load_scale_rows(nc.sync, tab_sc[32 * q : 32 * q + 16, :], tab_scales[:, 4 * q : 4 * q + 4, :])
+        tab_win[3] = load_words(tab_words, 3, "tab_win3")
+        w_rows[0, 1] = load_rows(w1[PASS : 2 * PASS, 0:PASS], "w1_rows01")
+        idx2 = load_list(offs2, "idx2")
+        for q in range(QUADS):
+            load_scale_rows(nc.sync, tab2_sc[32 * q + 8 : 32 * q + 16, :], tab2_scales[:, 4 * q : 4 * q + 4, :])
+        tab_win[0] = load_words(tab_words, 0, "tab_win0")
+        for q in range(QUADS):
+            load_scale_rows(nc.gpsimd, tab3_sc[32 * q + 8 : 32 * q + 16, :], tab3_scales[:, 4 * q : 4 * q + 4, :])
 
-        b1_sb = keep.tile([P, 2, PACK], F32, name="b1_sb")
         gain_sb = keep.tile([P, 2, PACK], F32, name="gain_sb")
         c2_sb = keep.tile([P, QUADS], F32, name="c2_sb")
-        nc.gpsimd.dma_start(out=b1_sb[:], in_=b1.rearrange("(b p i) -> p b i", p=P, i=PACK))
         nc.gpsimd.dma_start(out=gain_sb[:], in_=gain.rearrange("(b p i) -> p b i", p=P, i=PACK))
-        for tile, scales in ((tab2_sc, tab2_scales), (tab3_sc, tab3_scales)):
-            for q in range(QUADS):
-                load_scale_rows(nc.gpsimd, tile[32 * q + 8 : 32 * q + 16, :], scales[:, 4 * q : 4 * q + 4, :])
         with nc.allow_non_contiguous_dma(reason="one value of c2 for each partition and output tile"):
             nc.gpsimd.dma_start(out=c2_sb[:], in_=c2.rearrange("(m p) -> p m", p=P))
-
-        for a in (3, 0, 1):
-            tab_win[a] = load_words(tab_words, a)
-        w_rows[1, 0] = load_rows(w1[0:PASS, PASS : 2 * PASS])
-        w_rows[1, 1] = load_rows(w1[PASS : 2 * PASS, PASS : 2 * PASS])
-        tab2_win = [load_words(tab2_words, a) for a in range(2)]
-        res0 = load_rows(res[0:PASS, :])
-        tab3_win = [load_words(tab3_words, a) for a in range(2)]
-        res1 = [load_rows(res[PASS : 2 * PASS, jh * HALF : (jh + 1) * HALF]) for jh in range(2)]
 
         w1_codes, w1_scales = {}, {}
 
@@ -138,26 +129,42 @@ def tile_list_companion_introduction_score_kernel(
             w1_scales[b, a] = held([P, PASS], U8, "w1_scales%d%d" % (b, a))
             quantise(woven[:], w1_codes[b, a][:], w1_scales[b, a][:])
 
-        for a in range(2):
-            quantise_w1(round_w1(nc.scalar.copy, 0, a), 0, a)
-
-        w4_dealt = held([P, 2, H], U16, "w4_dealt")
-        nc.scalar.copy(
-            out=w4_dealt[:].rearrange("p a (b t m) -> p (a b) m t", b=2, t=PACK),
-            in_=w4_raw[:].rearrange("p a (b m t) -> p (a b) m t", b=2, t=PACK),
-        )
-
-        v_scales = [gather(tab_sc[:, s, :], idx, U8, "v_scales%d" % s) for s in range(2)]
-        v_codes = {}
-        for a in (2, 3):
-            v_codes[a] = gather(tab_win[a][:], idx, U32, "v_codes%d" % a)
+        v_codes = {2: gather(tab_win[2][:], idx, U32, "v_codes2")}
         w4_sc_dealt = held([P, 2, H], U8, "w4_sc_dealt")
         nc.vector.tensor_copy(
             out=w4_sc_dealt[:].rearrange("p a (b t m) -> p (a b) m t", b=2, t=PACK),
             in_=w4_sc[:].rearrange("p a (b m t) -> p (a b) m t", b=2, t=PACK),
         )
+        v_scales = gather(tab_sc[:], idx, U8, "v_scales")
+        quantise_w1(round_w1(nc.scalar.copy, 0, 0), 0, 0)
+        w4_dealt = held([P, 2, H], U16, "w4_dealt")
+        nc.scalar.copy(
+            out=w4_dealt[:].rearrange("p a (b t m) -> p (a b) m t", b=2, t=PACK),
+            in_=w4_raw[:].rearrange("p a (b m t) -> p (a b) m t", b=2, t=PACK),
+        )
+        v_codes[3] = gather(tab_win[3][:], idx, U32, "v_codes3")
+        v2_scales = gather(tab2_sc[:], idx2, U8, "v2_scales")
+        quantise_w1(round_w1(nc.scalar.copy, 0, 1), 0, 1)
+
+        tab_win[1] = load_words(tab_words, 1, "w4_then_tab")
+        idx3 = load_list(offs3, "idx3")
+        v_scales1 = held([P, S], U8, "v_scales1")
+        for q in range(QUADS):
+            load_scale_rows(nc.sync, v_scales1[32 * q : 32 * q + 4, :], v_scales[32 * q + 4 : 32 * q + 8, :])
+        v_planes = [v_scales[:], v_scales1[:], v_scales[8:P, :], v_scales[12:P, :]]
+        w_rows[1, 0] = load_rows(w1[0:PASS, PASS : 2 * PASS], "w1_rows10")
+        w_rows[1, 1] = load_rows(w1[PASS : 2 * PASS, PASS : 2 * PASS], "w1_rows11")
+        tab2_win = [load_words(tab2_words, 0, "tab2_win0")]
+        res0 = load_rows(res[0:PASS, :], "w1_then_res")
+        tab2_win.append(load_words(tab2_words, 1, "tab2_win1"))
+        tab3_win = [load_words(tab3_words, a, "tab3_win%d" % a) for a in range(2)]
+        res1 = [
+            load_rows(res[PASS : 2 * PASS, jh * HALF : (jh + 1) * HALF], "res1%d" % jh) for jh in range(2)
+        ]
+
         for a in (0, 1):
             v_codes[a] = gather(tab_win[a][:], idx, U32, "v_codes%d" % a)
+        v3_scales = gather(tab3_sc[:], idx3, U8, "w4_then_tab")
 
         def first_stage_pass(acc, b, a, start, stop):
             for i in range(PACK):
@@ -169,29 +176,31 @@ def tile_list_companion_introduction_score_kernel(
                     lhsT, lhsT_scale = w1_codes[b, a - 2][:, cols].bitcast(FP8X4), w1_scales[b, a - 2][:, cols]
                 nc.tensor.matmul_mx(
                     out=acc[i][:], lhsT=lhsT, lhsT_scale=lhsT_scale,
-                    rhs=v_codes[a][:].bitcast(FP8X4), rhs_scale=v_scales[a % 2][4 * (a // 2) : P, :],
+                    rhs=v_codes[a][:].bitcast(FP8X4), rhs_scale=v_planes[a],
                     start=start, stop=stop,
                 )
 
         y = [[bank(PACK * b + i) for i in range(PACK)] for b in range(2)]
         for n, a in enumerate((2, 3, 0, 1)):
             first_stage_pass(y[0], 0, a, n == 0, n == 3)
-        for a in (0, 1):
-            first_stage_pass(y[1], 1, a, a == 0, False)
+        for a in (1, 0):
+            first_stage_pass(y[1], 1, a, a == 1, False)
 
-        def first_result(b):
+        def gain_on_vector(h, t, g):
+            nc.vector.tensor_scalar(h, t, g, None, ALU.mult)
+
+        def gain_on_scalar(h, t, g):
+            nc.scalar.activation(out=h, in_=t, func=ACT.Copy, scale=g)
+
+        def first_result(b, apply_gain):
             h = held([P, PACK, S], F32, "h%d" % b)
-            for i in range(PACK):
-                t = ring([P, S], F32, "tanh", 3)
-                nc.scalar.activation(out=t[:], in_=y[b][i][:], func=ACT.Tanh, bias=b1_sb[:, b, i : i + 1])
-                nc.scalar.activation(out=h[:, i, :], in_=t[:], func=ACT.Copy, scale=gain_sb[:, b, i : i + 1])
+            t = [ring([P, S], F32, "tanh", PACK) for i in range(PACK)]
+            for step in range(PACK + 1):
+                if step < PACK:
+                    nc.scalar.activation(out=t[step][:], in_=y[b][step][:], func=ACT.Tanh, bias=b1_sb[:, b, step : step + 1])
+                if step > 0:
+                    apply_gain(h[:, step - 1, :], t[step - 1][:], gain_sb[:, b, step - 1 : step])
             return h
-
-        h0 = first_result(0)
-        for a in range(2):
-            quantise_w1(round_w1(nc.vector.tensor_copy, 1, a), 1, a)
-            first_stage_pass(y[1], 1, 2 + a, False, a == 1)
-        h1 = first_result(1)
 
         h_codes = [held([P, S], U32, "h_codes%d" % b) for b in range(2)]
         h_scales = [held([P, S], U8, "h_scales%d" % b) for b in range(2)]
@@ -199,25 +208,31 @@ def tile_list_companion_introduction_score_kernel(
         hr_codes1 = [held([P, HALF], U32, "hr_codes1%d" % jh) for jh in range(2)]
         hr_scales1 = [held([P, HALF], U8, "hr_scales1%d" % jh) for jh in range(2)]
 
-        def weave_h(h):
-            woven = ring([P, PACK * S], BF16, "woven", 3)
-            nc.vector.tensor_copy(out=by_lines_out(woven[:]), in_=by_lines_in(h[:]))
+        def weave_h(engine_copy, h_planes):
+            woven = ring([P, PACK * h_planes.shape[2]], BF16, "woven", 4)
+            engine_copy(out=by_lines_out(woven[:]), in_=by_lines_in(h_planes))
             return woven[:]
 
         def weave_hr(h_planes, res_planes):
             width = h_planes.shape[2]
-            woven = ring([P, PACK * width], BF16, "woven", 3)
+            woven = ring([P, PACK * width], BF16, "woven", 4)
             nc.vector.tensor_tensor(by_lines_out(woven[:]), by_lines_in(h_planes), by_lines_in(res_planes), ALU.add)
             return woven[:]
 
-        v2_scales = gather(tab2_sc[:], idx2, U8, "v2_scales")
-        woven = weave_h(h0)
+        for a in range(2):
+            quantise_w1(round_w1(nc.vector.tensor_copy, 1, a), 1, a)
+            first_stage_pass(y[1], 1, 2 + a, False, a == 1)
+        h0 = first_result(0, gain_on_vector)
+        woven_h0 = weave_h(nc.scalar.copy, h0[:])
+        h1 = first_result(1, gain_on_scalar)
+        woven_h1 = [weave_h(nc.vector.tensor_copy, h1[:, :, :HALF]), weave_h(nc.scalar.copy, h1[:, :, HALF:])]
+
         v2_codes = [gather(tab2_win[0][:], idx2, U32, "v2_codes0")]
-        quantise(woven, h_codes[0][:], h_scales[0][:])
+        quantise(woven_h0, h_codes[0][:], h_scales[0][:])
         v2_codes.append(gather(tab2_win[1][:], idx2, U32, "v2_codes1"))
-        woven = weave_h(h1)
-        v3_scales = gather(tab3_sc[:], idx3, U8, "v3_scales")
-        quantise(woven, h_codes[1][:], h_scales[1][:])
+        for jh in range(2):
+            members = slice(HALF * jh, HALF * (jh + 1))
+            quantise(woven_h1[jh], h_codes[1][:, members], h_scales[1][:, members])
 
         e2 = [bank(m) for m in range(QUADS)]
         for b in range(2):
@@ -228,50 +243,44 @@ def tile_list_companion_introduction_score_kernel(
                     rhs=h_codes[b][:].bitcast(FP8X4), rhs_scale=h_scales[b][:], start=b == 0, stop=b == 1,
                 )
 
-        u = held([P, QUADS, S], F32, "u")
-        for m in range(QUADS):
-            a = ring([P, S], F32, "angle", 2)
-            nc.scalar.activation(out=a[:], in_=e2[m][:], func=ACT.Sin, bias=phase[:], scale=0.25)
-            nc.scalar.activation(out=a[:], in_=a[:], func=ACT.Square)
-            nc.scalar.activation(out=u[:, m, :], in_=a[:], func=ACT.Square, bias=one[:], scale=-2.0)
+        u = [held([P, S], F32, "u%d" % m) for m in range(QUADS)]
+        for step in range(QUADS + 2):
+            if step < QUADS:
+                nc.scalar.activation(out=u[step][:], in_=e2[step][:], func=ACT.Sin, bias=phase[:], scale=0.25)
+            if 1 <= step <= QUADS:
+                nc.scalar.activation(out=u[step - 1][:], in_=u[step - 1][:], func=ACT.Square)
+            if step >= 2:
+                nc.scalar.activation(out=u[step - 2][:], in_=u[step - 2][:], func=ACT.Square, bias=1.0, scale=-2.0)
 
         woven = weave_hr(h0[:], res0[:])
         v3_codes = [gather(tab3_win[0][:], idx3, U32, "v3_codes0")]
         quantise(woven, hr_codes0[:], hr_scales0[:])
         v3_codes.append(gather(tab3_win[1][:], idx3, U32, "v3_codes1"))
 
-        e3 = {(jh, pair): bank(QUADS + 2 * jh + pair) for jh in range(2) for pair in range(2)}
+        e3 = [bank(QUADS + m) for m in range(QUADS)]
 
-        def second_pass(jh, b, codes, scales):
+        def outing_pass(b, members, codes, scales, start, stop):
             for m in range(QUADS):
                 cols = slice(P * m, P * (m + 1))
                 nc.tensor.matmul_mx(
-                    out=e3[jh, m // 2][:, HALF * (m % 2) : HALF * (m % 2 + 1)],
+                    out=e3[m][:, members],
                     lhsT=v3_codes[b][:, cols].bitcast(FP8X4), lhsT_scale=v3_scales[8 + 4 * b : P, cols],
-                    rhs=codes.bitcast(FP8X4), rhs_scale=scales,
-                    start=b == 0 and m % 2 == 0, stop=b == 1 and m % 2 == 1,
+                    rhs=codes.bitcast(FP8X4), rhs_scale=scales, start=start, stop=stop,
                 )
 
+        outing_pass(0, slice(0, S), hr_codes0[:], hr_scales0[:], True, False)
+        woven_hr1 = [weave_hr(h1[:, :, HALF * jh : HALF * (jh + 1)], res1[jh][:]) for jh in range(2)]
         for jh in range(2):
-            members = slice(HALF * jh, HALF * (jh + 1))
-            second_pass(jh, 0, hr_codes0[:, members], hr_scales0[:, members])
-        for jh in range(2):
-            members = slice(HALF * jh, HALF * (jh + 1))
-            woven = weave_hr(h1[:, :, members], res1[jh][:])
-            quantise(woven, hr_codes1[jh][:], hr_scales1[jh][:])
-            second_pass(jh, 1, hr_codes1[jh][:], hr_scales1[jh][:])
-        for jh in range(2):
-            members = slice(HALF * jh, HALF * (jh + 1))
-            for pair in range(2):
-                o = ring([P, 2, HALF], F32, "score", 4)
-                nc.vector.scalar_tensor_tensor(
-                    out=o[:], in0=u[:, 2 * pair : 2 * pair + 2, members], scalar=0.5,
-                    in1=e3[jh, pair][:].rearrange("p (m j) -> p m j", m=2), op0=ALU.subtract, op1=ALU.mult,
-                )
-                for m in range(2):
-                    nc.scalar.activation(
-                        out=o[:, m, :], in_=o[:, m, :], func=ACT.Identity,
-                        bias=c2_sb[:, 2 * pair + m : 2 * pair + m + 1], scale=2.0,
-                    )
-                rows = slice(2 * P * pair, 2 * P * (pair + 1))
-                nc.sync.dma_start(out=out[rows, members].rearrange("(m p) j -> p m j", p=P), in_=o[:])
+            quantise(woven_hr1[jh], hr_codes1[jh][:], hr_scales1[jh][:])
+            outing_pass(1, slice(HALF * jh, HALF * (jh + 1)), hr_codes1[jh][:], hr_scales1[jh][:], False, jh == 1)
+
+        for m in range(QUADS):
+            o = held([P, S], F32, "score%d" % m)
+            nc.vector.scalar_tensor_tensor(
+                out=o[:], in0=u[m][:], scalar=0.5, in1=e3[m][:], op0=ALU.subtract, op1=ALU.mult
+            )
+            if m < 2:
+                nc.gpsimd.tensor_scalar(o[:], o[:], 2.0, c2_sb[:, m : m + 1], ALU.mult, ALU.add)
+            else:
+                nc.scalar.activation(out=o[:], in_=o[:], func=ACT.Identity, bias=c2_sb[:, m : m + 1], scale=2.0)
+            nc.sync.dma_start(out=out[P * m : P * (m + 1), :], in_=o[:])

@@ -76,15 +76,15 @@ def tile_list_companion_introduction_score_kernel(
 
         tab_sc = held([P, T], U8, "tab_sc")
         w4_sc = held([P, 2, H], U8, "w4_sc")
-        tab2_sc = held([P, T], U8, "tab2_sc")
-        tab3_sc = held([P, T], U8, "tab3_sc")
+        tab2_sc = ring([P, T], U8, "scales2_then_codes", 1)
+        tab3_sc = ring([P, T], U8, "scales3_then_w1", 1)
         for tile in (w4_sc, tab_sc):
             nc.vector.memset(tile[:].bitcast(I32), 0)
         seed = ring([P, 1], F32, "seed_then_b1", 1)
         nc.vector.memset(seed[:], 1.0)
         phase = keep.tile([P, 1], F32, name="phase")
         nc.vector.tensor_scalar(phase[:], seed[:], -math.pi / 8, None, ALU.mult)
-        for tile in (tab3_sc, tab2_sc):
+        for tile in (tab2_sc, tab3_sc):
             nc.vector.memset(tile[:].bitcast(I32), 0)
 
         idx = load_list(offs, "idx")
@@ -102,11 +102,10 @@ def tile_list_companion_introduction_score_kernel(
         tab_win[3] = load_words(tab_words, 3, "tab_win3")
         w_rows[0, 1] = load_rows(w1[PASS : 2 * PASS, 0:PASS], "w1_rows01")
         idx2 = load_list(offs2, "idx2")
-        for q in range(QUADS):
-            load_scale_rows(nc.sync, tab2_sc[32 * q + 8 : 32 * q + 16, :], tab2_scales[:, 4 * q : 4 * q + 4, :])
         tab_win[0] = load_words(tab_words, 0, "tab_win0")
-        for q in range(QUADS):
-            load_scale_rows(nc.gpsimd, tab3_sc[32 * q + 8 : 32 * q + 16, :], tab3_scales[:, 4 * q : 4 * q + 4, :])
+        for tile, scales in ((tab2_sc, tab2_scales), (tab3_sc, tab3_scales)):
+            for q in range(QUADS):
+                load_scale_rows(nc.gpsimd, tile[32 * q + 8 : 32 * q + 16, :], scales[:, 4 * q : 4 * q + 4, :])
 
         gain_sb = keep.tile([P, 2, PACK], F32, name="gain_sb")
         c2_sb = keep.tile([P, QUADS], F32, name="c2_sb")
@@ -116,8 +115,8 @@ def tile_list_companion_introduction_score_kernel(
 
         w1_codes, w1_scales = {}, {}
 
-        def round_w1(engine_copy, b, a):
-            woven = ring([P, PACK * PASS], BF16, "w1_bf", 2)
+        def round_w1(engine_copy, b, a, slot):
+            woven = ring([P, PACK * PASS], BF16, slot, 1)
             engine_copy(
                 out=woven[:].rearrange("p (t m j) -> p m j t", t=PACK, j=PACK),
                 in_=w_rows[b, a][:].rearrange("p j (m t) -> p m j t", t=PACK),
@@ -136,15 +135,15 @@ def tile_list_companion_introduction_score_kernel(
             in_=w4_sc[:].rearrange("p a (b m t) -> p (a b) m t", b=2, t=PACK),
         )
         v_scales = gather(tab_sc[:], idx, U8, "v_scales")
-        quantise_w1(round_w1(nc.scalar.copy, 0, 0), 0, 0)
+        quantise_w1(round_w1(nc.scalar.copy, 0, 0, "w1_bf00"), 0, 0)
         w4_dealt = held([P, 2, H], U16, "w4_dealt")
         nc.scalar.copy(
             out=w4_dealt[:].rearrange("p a (b t m) -> p (a b) m t", b=2, t=PACK),
             in_=w4_raw[:].rearrange("p a (b m t) -> p (a b) m t", b=2, t=PACK),
         )
         v_codes[3] = gather(tab_win[3][:], idx, U32, "v_codes3")
-        v2_scales = gather(tab2_sc[:], idx2, U8, "v2_scales")
-        quantise_w1(round_w1(nc.scalar.copy, 0, 1), 0, 1)
+        v2_scales = gather(tab2_sc[:], idx2, U8, "tab_win3")
+        quantise_w1(round_w1(nc.scalar.copy, 0, 1, "w1_bf01"), 0, 1)
 
         tab_win[1] = load_words(tab_words, 1, "w4_then_tab")
         idx3 = load_list(offs3, "idx3")
@@ -162,8 +161,8 @@ def tile_list_companion_introduction_score_kernel(
             load_rows(res[PASS : 2 * PASS, jh * HALF : (jh + 1) * HALF], "res1%d" % jh) for jh in range(2)
         ]
 
-        for a in (0, 1):
-            v_codes[a] = gather(tab_win[a][:], idx, U32, "v_codes%d" % a)
+        v_codes[0] = gather(tab_win[0][:], idx, U32, "scales2_then_codes")
+        v_codes[1] = gather(tab_win[1][:], idx, U32, "tab_win0")
         v3_scales = gather(tab3_sc[:], idx3, U8, "w4_then_tab")
 
         def first_stage_pass(acc, b, a, start, stop):
@@ -186,21 +185,12 @@ def tile_list_companion_introduction_score_kernel(
         for a in (1, 0):
             first_stage_pass(y[1], 1, a, a == 1, False)
 
-        def gain_on_vector(h, t, g):
-            nc.vector.tensor_scalar(h, t, g, None, ALU.mult)
+        h = [held([P, PACK, S], F32, "h%d" % b) for b in range(2)]
 
-        def gain_on_scalar(h, t, g):
-            nc.scalar.activation(out=h, in_=t, func=ACT.Copy, scale=g)
-
-        def first_result(b, apply_gain):
-            h = held([P, PACK, S], F32, "h%d" % b)
-            t = [ring([P, S], F32, "tanh", PACK) for i in range(PACK)]
-            for step in range(PACK + 1):
-                if step < PACK:
-                    nc.scalar.activation(out=t[step][:], in_=y[b][step][:], func=ACT.Tanh, bias=b1_sb[:, b, step : step + 1])
-                if step > 0:
-                    apply_gain(h[:, step - 1, :], t[step - 1][:], gain_sb[:, b, step - 1 : step])
-            return h
+        def tanh_plane(b, i):
+            t = ring([P, S], F32, "tanh", PACK)
+            nc.scalar.activation(out=t[:], in_=y[b][i][:], func=ACT.Tanh, bias=b1_sb[:, b, i : i + 1])
+            return t
 
         h_codes = [held([P, S], U32, "h_codes%d" % b) for b in range(2)]
         h_scales = [held([P, S], U8, "h_scales%d" % b) for b in range(2)]
@@ -208,28 +198,42 @@ def tile_list_companion_introduction_score_kernel(
         hr_codes1 = [held([P, HALF], U32, "hr_codes1%d" % jh) for jh in range(2)]
         hr_scales1 = [held([P, HALF], U8, "hr_scales1%d" % jh) for jh in range(2)]
 
-        def weave_h(engine_copy, h_planes):
-            woven = ring([P, PACK * h_planes.shape[2]], BF16, "woven", 4)
-            engine_copy(out=by_lines_out(woven[:]), in_=by_lines_in(h_planes))
+        def weave_h(h_planes, slot):
+            woven = ring([P, PACK * h_planes.shape[2]], BF16, slot, 1)
+            nc.scalar.copy(out=by_lines_out(woven[:]), in_=by_lines_in(h_planes))
             return woven[:]
 
-        def weave_hr(h_planes, res_planes):
-            width = h_planes.shape[2]
-            woven = ring([P, PACK * width], BF16, "woven", 4)
+        def weave_hr(h_planes, res_planes, slot):
+            woven = ring([P, PACK * h_planes.shape[2]], BF16, slot, 1)
             nc.vector.tensor_tensor(by_lines_out(woven[:]), by_lines_in(h_planes), by_lines_in(res_planes), ALU.add)
             return woven[:]
 
-        for a in range(2):
-            quantise_w1(round_w1(nc.vector.tensor_copy, 1, a), 1, a)
-            first_stage_pass(y[1], 1, 2 + a, False, a == 1)
-        h0 = first_result(0, gain_on_vector)
-        woven_h0 = weave_h(nc.scalar.copy, h0[:])
-        h1 = first_result(1, gain_on_scalar)
-        woven_h1 = [weave_h(nc.vector.tensor_copy, h1[:, :, :HALF]), weave_h(nc.scalar.copy, h1[:, :, HALF:])]
+        t = [tanh_plane(0, i) for i in range(PACK)]
+        woven = round_w1(nc.vector.tensor_copy, 1, 0, "scales3_then_w1")
+        for i in range(PACK):
+            nc.vector.tensor_scalar(h[0][:, i, :], t[i][:], gain_sb[:, 0, i : i + 1], None, ALU.mult)
+            if i == 0:
+                quantise_w1(woven, 1, 0)
+        first_stage_pass(y[1], 1, 2, False, False)
+        woven_h0 = weave_h(h[0][:], "woven_h0")
+        quantise_w1(round_w1(nc.vector.tensor_copy, 1, 1, "scales3_then_w1"), 1, 1)
+        first_stage_pass(y[1], 1, 3, False, True)
 
-        v2_codes = [gather(tab2_win[0][:], idx2, U32, "v2_codes0")]
+        t = []
+        for step in range(PACK + 1):
+            if step < PACK:
+                t.append(tanh_plane(1, step))
+            if step > 0:
+                i = step - 1
+                nc.scalar.activation(out=h[1][:, i, :], in_=t[i][:], func=ACT.Copy, scale=gain_sb[:, 1, i : i + 1])
+        woven_h1 = [weave_h(h[1][:, :, HALF * jh : HALF * (jh + 1)], "woven_h1%d" % jh) for jh in range(2)]
+
+        v2_codes = [gather(tab2_win[0][:], idx2, U32, "scales3_then_w1")]
         quantise(woven_h0, h_codes[0][:], h_scales[0][:])
-        v2_codes.append(gather(tab2_win[1][:], idx2, U32, "v2_codes1"))
+        woven = weave_hr(h[0][:], res0[:], "woven_h0")
+        v2_codes.append(gather(tab2_win[1][:], idx2, U32, "w1_then_res"))
+        quantise(woven, hr_codes0[:], hr_scales0[:])
+        v3_codes = [gather(tab3_win[0][:], idx3, U32, "woven_h0")]
         for jh in range(2):
             members = slice(HALF * jh, HALF * (jh + 1))
             quantise(woven_h1[jh], h_codes[1][:, members], h_scales[1][:, members])
@@ -252,10 +256,7 @@ def tile_list_companion_introduction_score_kernel(
             if step >= 2:
                 nc.scalar.activation(out=u[step - 2][:], in_=u[step - 2][:], func=ACT.Square, bias=1.0, scale=-2.0)
 
-        woven = weave_hr(h0[:], res0[:])
-        v3_codes = [gather(tab3_win[0][:], idx3, U32, "v3_codes0")]
-        quantise(woven, hr_codes0[:], hr_scales0[:])
-        v3_codes.append(gather(tab3_win[1][:], idx3, U32, "v3_codes1"))
+        v3_codes.append(gather(tab3_win[1][:], idx3, U32, "woven_h11"))
 
         e3 = [bank(QUADS + m) for m in range(QUADS)]
 
@@ -269,18 +270,22 @@ def tile_list_companion_introduction_score_kernel(
                 )
 
         outing_pass(0, slice(0, S), hr_codes0[:], hr_scales0[:], True, False)
-        woven_hr1 = [weave_hr(h1[:, :, HALF * jh : HALF * (jh + 1)], res1[jh][:]) for jh in range(2)]
+        woven_hr1 = [
+            weave_hr(h[1][:, :, HALF * jh : HALF * (jh + 1)], res1[jh][:], ("tab3_win1", "woven_h10")[jh]) for jh in range(2)
+        ]
         for jh in range(2):
             quantise(woven_hr1[jh], hr_codes1[jh][:], hr_scales1[jh][:])
             outing_pass(1, slice(HALF * jh, HALF * (jh + 1)), hr_codes1[jh][:], hr_scales1[jh][:], False, jh == 1)
 
-        for m in range(QUADS):
-            o = held([P, S], F32, "score%d" % m)
+        pieces = [(m, slice(0, S)) for m in range(QUADS - 1)]
+        pieces += [(QUADS - 1, slice(HALF * jh, HALF * (jh + 1))) for jh in range(2)]
+        for n, (m, members) in enumerate(pieces):
+            o = held([P, members.stop - members.start], F32, "score%d" % n)
             nc.vector.scalar_tensor_tensor(
-                out=o[:], in0=u[m][:], scalar=0.5, in1=e3[m][:], op0=ALU.subtract, op1=ALU.mult
+                out=o[:], in0=u[m][:, members], scalar=0.5, in1=e3[m][:, members], op0=ALU.subtract, op1=ALU.mult
             )
             if m < 2:
                 nc.gpsimd.tensor_scalar(o[:], o[:], 2.0, c2_sb[:, m : m + 1], ALU.mult, ALU.add)
             else:
                 nc.scalar.activation(out=o[:], in_=o[:], func=ACT.Identity, bias=c2_sb[:, m : m + 1], scale=2.0)
-            nc.sync.dma_start(out=out[P * m : P * (m + 1), :], in_=o[:])
+            nc.sync.dma_start(out=out[P * m : P * (m + 1), members], in_=o[:])

@@ -3,7 +3,7 @@ from contextlib import ExitStack
 
 import concourse.mybir as mybir
 
-K, KA, KB, H, T, S, S2 = 2048, 1024, 1024, 1024, 2048, 512, 512
+K, H, T, S, S2 = 2048, 1024, 2048, 512, 512
 FLOPS = 2 * (K * H * S + 2 * H * S2 * S)
 
 F32 = mybir.dt.float32
@@ -21,7 +21,14 @@ P = 128
 PACK = 4
 PASS = P * PACK
 QUADS = 4
+QUAD = P // QUADS
+ROWS = 4
+LINE = 4
+UPPER = 2 * ROWS
+M_TILES = S2 // P
+ADDS_ON_GPSIMD = 2
 HALF = S // 2
+HALVES = [slice(0, HALF), slice(HALF, S)]
 
 
 def tile_list_companion_introduction_score_kernel(
@@ -36,8 +43,8 @@ def tile_list_companion_introduction_score_kernel(
         def held(shape, dtype, name):
             return keep.tile(shape, dtype, name=name, align_bytes=64)
 
-        def ring(shape, dtype, tag, bufs):
-            return keep.tile(shape, dtype, name=tag, tag=tag, bufs=bufs, align_bytes=64)
+        def in_slot(shape, dtype, slot, bufs=1):
+            return keep.tile(shape, dtype, name=slot, tag=slot, bufs=bufs, align_bytes=64)
 
         def bank(n):
             return psum.tile([P, S], F32, name="bank%d" % n, tag="bank%d" % n)
@@ -48,39 +55,45 @@ def tile_list_companion_introduction_score_kernel(
             return tile
 
         def load_words(words, a, slot):
-            tile = ring([P, T], U32, slot, 1)
+            tile = in_slot([P, T], U32, slot)
             nc.sync.dma_start(out=tile[:].bitcast(I32), in_=words[a].rearrange("p t i -> p (t i)").bitcast(I32))
             return tile
 
         def load_rows(rows, slot):
-            tile = ring([P, PACK, rows.shape[1]], F32, slot, 1)
+            tile = in_slot([P, PACK, rows.shape[1]], F32, slot)
             nc.sync.dma_start(out=tile[:], in_=rows.rearrange("(p i) c -> p i c", i=PACK))
             return tile
 
-        def gather(window, offsets, dtype, name):
-            tile = ring([P, S], dtype, name, 1)
+        def move_scale_rows(queue, to_rows, from_rows):
+            queue.dma_start(out=to_rows.bitcast(I32), in_=from_rows.bitcast(I32))
+
+        def gather(window, offsets, dtype, slot):
+            tile = in_slot([P, S], dtype, slot)
             nc.vector.tensor_copy(tile[:], window.indirect(offsets[:]))
             return tile
 
-        def quantise(values, codes, scales):
-            nc.vector.quantize_mx(out=codes.bitcast(FP8X4), scales=scales, in_=values)
+        def quantise(woven, codes, scales):
+            nc.vector.quantize_mx(out=codes.bitcast(FP8X4), scales=scales, in_=woven)
 
-        def by_lines_in(planes):
-            return planes.rearrange("p i (c e) -> p c i e", e=4)
+        def sets_by_lines(row_sets):
+            return row_sets.rearrange("p i (c e) -> p c i e", e=LINE)
 
-        def by_lines_out(woven):
-            return woven.rearrange("p (c e i) -> p c i e", e=4, i=PACK)
+        def woven_by_lines(woven):
+            return woven.rearrange("p (c e i) -> p c i e", e=LINE, i=PACK)
 
-        def load_scale_rows(queue, tile_rows, rows):
-            queue.dma_start(out=tile_rows.bitcast(I32), in_=rows.bitcast(I32))
+        def as_loaded(columns):
+            return columns.rearrange("p a (b m i) -> p (a b) m i", b=2, i=PACK)
+
+        def as_dealt(places):
+            return places.rearrange("p a (b i m) -> p (a b) m i", b=2, i=PACK)
 
         tab_sc = held([P, T], U8, "tab_sc")
         w4_sc = held([P, 2, H], U8, "w4_sc")
-        tab2_sc = ring([P, T], U8, "scales2_then_codes", 1)
-        tab3_sc = ring([P, T], U8, "scales3_then_w1", 1)
+        tab2_sc = in_slot([P, T], U8, "scales2_then_codes")
+        tab3_sc = in_slot([P, T], U8, "scales3_then_w1")
         for tile in (w4_sc, tab_sc):
             nc.vector.memset(tile[:].bitcast(I32), 0)
-        seed = ring([P, 1], F32, "seed_then_b1", 1)
+        seed = in_slot([P, 1], F32, "seed_then_b1")
         nc.vector.memset(seed[:], 1.0)
         phase = keep.tile([P, 1], F32, name="phase")
         nc.vector.tensor_scalar(phase[:], seed[:], -math.pi / 8, None, ALU.mult)
@@ -89,37 +102,39 @@ def tile_list_companion_introduction_score_kernel(
 
         idx = load_list(offs, "idx")
         tab_win = {2: load_words(tab_words, 2, "tab_win2")}
-        b1_sb = ring([P, 2, PACK], F32, "seed_then_b1", 1)
+        b1_sb = in_slot([P, 2, PACK], F32, "seed_then_b1")
         nc.sync.dma_start(out=b1_sb[:], in_=b1.rearrange("(b p i) -> p b i", p=P, i=PACK))
         for q in range(QUADS):
-            load_scale_rows(nc.sync, w4_sc[32 * q : 32 * q + 4, :, :], w4_scales[:, 4 * q : 4 * q + 4, :].rearrange("a r c -> r a c"))
-        w_rows = {}
-        w_rows[0, 0] = load_rows(w1[0:PASS, 0:PASS], "w1_then_res")
-        w4_raw = ring([P, 2, H], U16, "w4_then_tab", 1)
+            rows = w4_scales[:, ROWS * q : ROWS * (q + 1), :].rearrange("a r c -> r a c")
+            move_scale_rows(nc.sync, w4_sc[QUAD * q : QUAD * q + ROWS, :, :], rows)
+        w1_rows = {(0, 0): load_rows(w1[0:PASS, 0:PASS], "w1_then_res")}
+        w4_raw = in_slot([P, 2, H], U16, "w4_then_tab")
         nc.sync.dma_start(out=w4_raw[:].bitcast(I32), in_=w4_words.rearrange("a p c -> p a c").bitcast(I32))
         for q in range(QUADS):
-            load_scale_rows(nc.sync, tab_sc[32 * q : 32 * q + 16, :], tab_scales[:, 4 * q : 4 * q + 4, :])
+            move_scale_rows(
+                nc.sync, tab_sc[QUAD * q : QUAD * q + 4 * ROWS, :], tab_scales[:, ROWS * q : ROWS * (q + 1), :]
+            )
         tab_win[3] = load_words(tab_words, 3, "tab_win3")
-        w_rows[0, 1] = load_rows(w1[PASS : 2 * PASS, 0:PASS], "w1_rows01")
+        w1_rows[0, 1] = load_rows(w1[PASS : 2 * PASS, 0:PASS], "w1_rows01")
         idx2 = load_list(offs2, "idx2")
+        gain_sb = keep.tile([P, 2, PACK], F32, name="gain_sb")
+        nc.sync.dma_start(out=gain_sb[:], in_=gain.rearrange("(b p i) -> p b i", p=P, i=PACK))
         tab_win[0] = load_words(tab_words, 0, "tab_win0")
         for tile, scales in ((tab2_sc, tab2_scales), (tab3_sc, tab3_scales)):
             for q in range(QUADS):
-                load_scale_rows(nc.gpsimd, tile[32 * q + 8 : 32 * q + 16, :], scales[:, 4 * q : 4 * q + 4, :])
-
-        gain_sb = keep.tile([P, 2, PACK], F32, name="gain_sb")
-        c2_sb = keep.tile([P, QUADS], F32, name="c2_sb")
-        nc.gpsimd.dma_start(out=gain_sb[:], in_=gain.rearrange("(b p i) -> p b i", p=P, i=PACK))
-        with nc.allow_non_contiguous_dma(reason="one value of c2 for each partition and output tile"):
-            nc.gpsimd.dma_start(out=c2_sb[:], in_=c2.rearrange("(m p) -> p m", p=P))
+                move_scale_rows(
+                    nc.gpsimd,
+                    tile[QUAD * q + UPPER : QUAD * q + UPPER + 2 * ROWS, :],
+                    scales[:, ROWS * q : ROWS * (q + 1), :],
+                )
 
         w1_codes, w1_scales = {}, {}
 
         def round_w1(engine_copy, b, a, slot):
-            woven = ring([P, PACK * PASS], BF16, slot, 1)
+            woven = in_slot([P, PACK * PASS], BF16, slot)
             engine_copy(
-                out=woven[:].rearrange("p (t m j) -> p m j t", t=PACK, j=PACK),
-                in_=w_rows[b, a][:].rearrange("p j (m t) -> p m j t", t=PACK),
+                out=woven[:].rearrange("p (i m j) -> p m j i", i=PACK, j=PACK),
+                in_=w1_rows[b, a][:].rearrange("p j (m i) -> p m j i", i=PACK),
             )
             return woven
 
@@ -130,17 +145,11 @@ def tile_list_companion_introduction_score_kernel(
 
         v_codes = {2: gather(tab_win[2][:], idx, U32, "v_codes2")}
         w4_sc_dealt = held([P, 2, H], U8, "w4_sc_dealt")
-        nc.vector.tensor_copy(
-            out=w4_sc_dealt[:].rearrange("p a (b t m) -> p (a b) m t", b=2, t=PACK),
-            in_=w4_sc[:].rearrange("p a (b m t) -> p (a b) m t", b=2, t=PACK),
-        )
+        nc.vector.tensor_copy(out=as_dealt(w4_sc_dealt[:]), in_=as_loaded(w4_sc[:]))
         v_scales = gather(tab_sc[:], idx, U8, "v_scales")
         quantise_w1(round_w1(nc.scalar.copy, 0, 0, "w1_bf00"), 0, 0)
         w4_dealt = held([P, 2, H], U16, "w4_dealt")
-        nc.scalar.copy(
-            out=w4_dealt[:].rearrange("p a (b t m) -> p (a b) m t", b=2, t=PACK),
-            in_=w4_raw[:].rearrange("p a (b m t) -> p (a b) m t", b=2, t=PACK),
-        )
+        nc.scalar.copy(out=as_dealt(w4_dealt[:]), in_=as_loaded(w4_raw[:]))
         v_codes[3] = gather(tab_win[3][:], idx, U32, "v_codes3")
         v2_scales = gather(tab2_sc[:], idx2, U8, "tab_win3")
         quantise_w1(round_w1(nc.scalar.copy, 0, 1, "w1_bf01"), 0, 1)
@@ -149,48 +158,52 @@ def tile_list_companion_introduction_score_kernel(
         idx3 = load_list(offs3, "idx3")
         v_scales1 = held([P, S], U8, "v_scales1")
         for q in range(QUADS):
-            load_scale_rows(nc.sync, v_scales1[32 * q : 32 * q + 4, :], v_scales[32 * q + 4 : 32 * q + 8, :])
-        v_planes = [v_scales[:], v_scales1[:], v_scales[8:P, :], v_scales[12:P, :]]
-        w_rows[1, 0] = load_rows(w1[0:PASS, PASS : 2 * PASS], "w1_rows10")
-        w_rows[1, 1] = load_rows(w1[PASS : 2 * PASS, PASS : 2 * PASS], "w1_rows11")
+            move_scale_rows(
+                nc.sync, v_scales1[QUAD * q : QUAD * q + ROWS, :], v_scales[QUAD * q + ROWS : QUAD * q + 2 * ROWS, :]
+            )
+        v_planes = [v_scales[:], v_scales1[:], v_scales[2 * ROWS : P, :], v_scales[3 * ROWS : P, :]]
+        w1_rows[1, 0] = load_rows(w1[0:PASS, PASS : 2 * PASS], "w1_rows10")
+        w1_rows[1, 1] = load_rows(w1[PASS : 2 * PASS, PASS : 2 * PASS], "w1_rows11")
         tab2_win = [load_words(tab2_words, 0, "tab2_win0")]
         res0 = load_rows(res[0:PASS, :], "w1_then_res")
         tab2_win.append(load_words(tab2_words, 1, "tab2_win1"))
         tab3_win = [load_words(tab3_words, a, "tab3_win%d" % a) for a in range(2)]
-        res1 = [
-            load_rows(res[PASS : 2 * PASS, jh * HALF : (jh + 1) * HALF], "res1%d" % jh) for jh in range(2)
-        ]
+        res1 = [load_rows(res[PASS : 2 * PASS, HALVES[jh]], "res1%d" % jh) for jh in range(2)]
+        c2_sb = keep.tile([P, M_TILES], F32, name="c2_sb")
+        with nc.allow_non_contiguous_dma(reason="one value of c2 for each partition and output tile"):
+            nc.sync.dma_start(out=c2_sb[:], in_=c2.rearrange("(m p) -> p m", p=P))
 
         v_codes[0] = gather(tab_win[0][:], idx, U32, "scales2_then_codes")
         v_codes[1] = gather(tab_win[1][:], idx, U32, "tab_win0")
         v3_scales = gather(tab3_sc[:], idx3, U8, "w4_then_tab")
 
-        def first_stage_pass(acc, b, a, start, stop):
+        y = [[bank(PACK * b + i) for i in range(PACK)] for b in range(2)]
+
+        def first_stage_pass(b, a, start, stop):
             for i in range(PACK):
                 if a < 2:
-                    cols = slice(PASS * b + P * i, PASS * b + P * (i + 1))
-                    lhsT, lhsT_scale = w4_dealt[:, a, cols].bitcast(FP4X4), w4_sc_dealt[:, a, cols]
+                    places = slice(PASS * b + P * i, PASS * b + P * (i + 1))
+                    lhsT, lhsT_scale = w4_dealt[:, a, places].bitcast(FP4X4), w4_sc_dealt[:, a, places]
                 else:
-                    cols = slice(P * i, P * (i + 1))
-                    lhsT, lhsT_scale = w1_codes[b, a - 2][:, cols].bitcast(FP8X4), w1_scales[b, a - 2][:, cols]
+                    places = slice(P * i, P * (i + 1))
+                    lhsT, lhsT_scale = w1_codes[b, a - 2][:, places].bitcast(FP8X4), w1_scales[b, a - 2][:, places]
                 nc.tensor.matmul_mx(
-                    out=acc[i][:], lhsT=lhsT, lhsT_scale=lhsT_scale,
+                    out=y[b][i][:], lhsT=lhsT, lhsT_scale=lhsT_scale,
                     rhs=v_codes[a][:].bitcast(FP8X4), rhs_scale=v_planes[a],
                     start=start, stop=stop,
                 )
 
-        y = [[bank(PACK * b + i) for i in range(PACK)] for b in range(2)]
-        for n, a in enumerate((2, 3, 0, 1)):
-            first_stage_pass(y[0], 0, a, n == 0, n == 3)
+        for a in (2, 3, 0, 1):
+            first_stage_pass(0, a, start=a == 2, stop=a == 1)
         for a in (1, 0):
-            first_stage_pass(y[1], 1, a, a == 1, False)
+            first_stage_pass(1, a, start=a == 1, stop=False)
 
         h = [held([P, PACK, S], F32, "h%d" % b) for b in range(2)]
 
-        def tanh_plane(b, i):
-            t = ring([P, S], F32, "tanh", PACK)
-            nc.scalar.activation(out=t[:], in_=y[b][i][:], func=ACT.Tanh, bias=b1_sb[:, b, i : i + 1])
-            return t
+        def tanh_of_set(b, i):
+            tile = in_slot([P, S], F32, "tanh", bufs=PACK)
+            nc.scalar.activation(out=tile[:], in_=y[b][i][:], func=ACT.Tanh, bias=b1_sb[:, b, i : i + 1])
+            return tile
 
         h_codes = [held([P, S], U32, "h_codes%d" % b) for b in range(2)]
         h_scales = [held([P, S], U8, "h_scales%d" % b) for b in range(2)]
@@ -198,94 +211,93 @@ def tile_list_companion_introduction_score_kernel(
         hr_codes1 = [held([P, HALF], U32, "hr_codes1%d" % jh) for jh in range(2)]
         hr_scales1 = [held([P, HALF], U8, "hr_scales1%d" % jh) for jh in range(2)]
 
-        def weave_h(h_planes, slot):
-            woven = ring([P, PACK * h_planes.shape[2]], BF16, slot, 1)
-            nc.scalar.copy(out=by_lines_out(woven[:]), in_=by_lines_in(h_planes))
+        def weave_h(h_sets, slot):
+            woven = in_slot([P, PACK * h_sets.shape[2]], BF16, slot)
+            nc.scalar.copy(out=woven_by_lines(woven[:]), in_=sets_by_lines(h_sets))
             return woven[:]
 
-        def weave_hr(h_planes, res_planes, slot):
-            woven = ring([P, PACK * h_planes.shape[2]], BF16, slot, 1)
-            nc.vector.tensor_tensor(by_lines_out(woven[:]), by_lines_in(h_planes), by_lines_in(res_planes), ALU.add)
+        def weave_hr(h_sets, res_sets, slot):
+            woven = in_slot([P, PACK * h_sets.shape[2]], BF16, slot)
+            nc.vector.tensor_tensor(woven_by_lines(woven[:]), sets_by_lines(h_sets), sets_by_lines(res_sets), ALU.add)
             return woven[:]
 
-        t = [tanh_plane(0, i) for i in range(PACK)]
-        woven = round_w1(nc.vector.tensor_copy, 1, 0, "scales3_then_w1")
+        tanh0 = [tanh_of_set(0, i) for i in range(PACK)]
+        woven_w1 = round_w1(nc.vector.tensor_copy, 1, 0, "scales3_then_w1")
         for i in range(PACK):
-            nc.vector.tensor_scalar(h[0][:, i, :], t[i][:], gain_sb[:, 0, i : i + 1], None, ALU.mult)
+            nc.vector.tensor_scalar(h[0][:, i, :], tanh0[i][:], gain_sb[:, 0, i : i + 1], None, ALU.mult)
             if i == 0:
-                quantise_w1(woven, 1, 0)
-        first_stage_pass(y[1], 1, 2, False, False)
+                quantise_w1(woven_w1, 1, 0)
+        first_stage_pass(1, 2, start=False, stop=False)
         woven_h0 = weave_h(h[0][:], "woven_h0")
         quantise_w1(round_w1(nc.vector.tensor_copy, 1, 1, "scales3_then_w1"), 1, 1)
-        first_stage_pass(y[1], 1, 3, False, True)
+        first_stage_pass(1, 3, start=False, stop=True)
 
-        t = []
+        tanh1 = []
         for step in range(PACK + 1):
             if step < PACK:
-                t.append(tanh_plane(1, step))
+                tanh1.append(tanh_of_set(1, step))
             if step > 0:
                 i = step - 1
-                nc.scalar.activation(out=h[1][:, i, :], in_=t[i][:], func=ACT.Copy, scale=gain_sb[:, 1, i : i + 1])
-        woven_h1 = [weave_h(h[1][:, :, HALF * jh : HALF * (jh + 1)], "woven_h1%d" % jh) for jh in range(2)]
+                nc.scalar.activation(out=h[1][:, i, :], in_=tanh1[i][:], func=ACT.Copy, scale=gain_sb[:, 1, i : i + 1])
+        woven_h1 = [weave_h(h[1][:, :, HALVES[jh]], "woven_h1%d" % jh) for jh in range(2)]
 
         v2_codes = [gather(tab2_win[0][:], idx2, U32, "scales3_then_w1")]
         quantise(woven_h0, h_codes[0][:], h_scales[0][:])
-        woven = weave_hr(h[0][:], res0[:], "woven_h0")
+        woven_hr0 = weave_hr(h[0][:], res0[:], "woven_h0")
         v2_codes.append(gather(tab2_win[1][:], idx2, U32, "w1_then_res"))
-        quantise(woven, hr_codes0[:], hr_scales0[:])
+        quantise(woven_hr0, hr_codes0[:], hr_scales0[:])
         v3_codes = [gather(tab3_win[0][:], idx3, U32, "woven_h0")]
         for jh in range(2):
-            members = slice(HALF * jh, HALF * (jh + 1))
-            quantise(woven_h1[jh], h_codes[1][:, members], h_scales[1][:, members])
+            quantise(woven_h1[jh], h_codes[1][:, HALVES[jh]], h_scales[1][:, HALVES[jh]])
 
-        e2 = [bank(m) for m in range(QUADS)]
+        e2 = [bank(m) for m in range(M_TILES)]
         for b in range(2):
-            for m in range(QUADS):
+            for m in range(M_TILES):
                 cols = slice(P * m, P * (m + 1))
                 nc.tensor.matmul_mx(
-                    out=e2[m][:], lhsT=v2_codes[b][:, cols].bitcast(FP8X4), lhsT_scale=v2_scales[8 + 4 * b : P, cols],
+                    out=e2[m][:],
+                    lhsT=v2_codes[b][:, cols].bitcast(FP8X4), lhsT_scale=v2_scales[UPPER + ROWS * b : P, cols],
                     rhs=h_codes[b][:].bitcast(FP8X4), rhs_scale=h_scales[b][:], start=b == 0, stop=b == 1,
                 )
 
-        u = [held([P, S], F32, "u%d" % m) for m in range(QUADS)]
-        for step in range(QUADS + 2):
-            if step < QUADS:
+        u = [held([P, S], F32, "u%d" % m) for m in range(M_TILES)]
+        for step in range(M_TILES + 2):
+            if step < M_TILES:
                 nc.scalar.activation(out=u[step][:], in_=e2[step][:], func=ACT.Sin, bias=phase[:], scale=0.25)
-            if 1 <= step <= QUADS:
+            if 1 <= step <= M_TILES:
                 nc.scalar.activation(out=u[step - 1][:], in_=u[step - 1][:], func=ACT.Square)
             if step >= 2:
                 nc.scalar.activation(out=u[step - 2][:], in_=u[step - 2][:], func=ACT.Square, bias=1.0, scale=-2.0)
 
         v3_codes.append(gather(tab3_win[1][:], idx3, U32, "woven_h11"))
 
-        e3 = [bank(QUADS + m) for m in range(QUADS)]
+        e3 = [bank(PACK + m) for m in range(M_TILES)]
 
         def outing_pass(b, members, codes, scales, start, stop):
-            for m in range(QUADS):
+            for m in range(M_TILES):
                 cols = slice(P * m, P * (m + 1))
                 nc.tensor.matmul_mx(
                     out=e3[m][:, members],
-                    lhsT=v3_codes[b][:, cols].bitcast(FP8X4), lhsT_scale=v3_scales[8 + 4 * b : P, cols],
+                    lhsT=v3_codes[b][:, cols].bitcast(FP8X4), lhsT_scale=v3_scales[UPPER + ROWS * b : P, cols],
                     rhs=codes.bitcast(FP8X4), rhs_scale=scales, start=start, stop=stop,
                 )
 
-        outing_pass(0, slice(0, S), hr_codes0[:], hr_scales0[:], True, False)
+        outing_pass(0, slice(0, S), hr_codes0[:], hr_scales0[:], start=True, stop=False)
         woven_hr1 = [
-            weave_hr(h[1][:, :, HALF * jh : HALF * (jh + 1)], res1[jh][:], ("tab3_win1", "woven_h10")[jh]) for jh in range(2)
+            weave_hr(h[1][:, :, HALVES[jh]], res1[jh][:], ("tab3_win1", "woven_h10")[jh]) for jh in range(2)
         ]
         for jh in range(2):
             quantise(woven_hr1[jh], hr_codes1[jh][:], hr_scales1[jh][:])
-            outing_pass(1, slice(HALF * jh, HALF * (jh + 1)), hr_codes1[jh][:], hr_scales1[jh][:], False, jh == 1)
+            outing_pass(1, HALVES[jh], hr_codes1[jh][:], hr_scales1[jh][:], start=False, stop=jh == 1)
 
-        pieces = [(m, slice(0, S)) for m in range(QUADS - 1)]
-        pieces += [(QUADS - 1, slice(HALF * jh, HALF * (jh + 1))) for jh in range(2)]
+        pieces = [(m, slice(0, S)) for m in range(M_TILES - 1)] + [(M_TILES - 1, members) for members in HALVES]
         for n, (m, members) in enumerate(pieces):
-            o = held([P, members.stop - members.start], F32, "score%d" % n)
+            score = held([P, members.stop - members.start], F32, "score%d" % n)
             nc.vector.scalar_tensor_tensor(
-                out=o[:], in0=u[m][:, members], scalar=0.5, in1=e3[m][:, members], op0=ALU.subtract, op1=ALU.mult
+                out=score[:], in0=u[m][:, members], scalar=0.5, in1=e3[m][:, members], op0=ALU.subtract, op1=ALU.mult
             )
-            if m < 2:
-                nc.gpsimd.tensor_scalar(o[:], o[:], 2.0, c2_sb[:, m : m + 1], ALU.mult, ALU.add)
+            if m < ADDS_ON_GPSIMD:
+                nc.gpsimd.tensor_scalar(score[:], score[:], 2.0, c2_sb[:, m : m + 1], ALU.mult, ALU.add)
             else:
-                nc.scalar.activation(out=o[:], in_=o[:], func=ACT.Identity, bias=c2_sb[:, m : m + 1], scale=2.0)
-            nc.sync.dma_start(out=out[P * m : P * (m + 1), members], in_=o[:])
+                nc.scalar.activation(out=score[:], in_=score[:], func=ACT.Identity, bias=c2_sb[:, m : m + 1], scale=2.0)
+            nc.sync.dma_start(out=out[P * m : P * (m + 1), members], in_=score[:])

import math
from contextlib import ExitStack

import concourse.mybir as mybir

K, H, T, S, S2 = 2048, 1024, 2048, 512, 512
FLOPS = 2 * (K * H * S + 2 * H * S2 * S)

F32 = mybir.dt.float32
BF16 = mybir.dt.bfloat16
I32 = mybir.dt.int32
U32 = mybir.dt.uint32
U16 = mybir.dt.uint16
U8 = mybir.dt.uint8
FP8X4 = mybir.dt.float8_e4m3fn_x4
FP4X4 = mybir.dt.float4_e2m1fn_x4
ACT = mybir.ActivationFunctionType
ALU = mybir.AluOpType

P = 128
PACK = 4
PASS = P * PACK
QUADS = 4
QUAD = P // QUADS
ROWS = 4
LINE = 4
UPPER = 2 * ROWS
M_TILES = S2 // P
ADDS_ON_GPSIMD = 2
HALF = S // 2
HALVES = [slice(0, HALF), slice(HALF, S)]


def tile_list_companion_introduction_score_kernel(
    tc, tab_words, tab_scales, tab2_words, tab2_scales, tab3_words, tab3_scales,
    w4_words, w4_scales, w1, b1, gain, res, c2, offs, offs2, offs3, out,
):
    nc = tc.nc
    with ExitStack() as ctx:
        keep = ctx.enter_context(tc.tile_pool(name="keep", bufs=1))
        psum = ctx.enter_context(tc.psum_pool(name="psum", bufs=1))

        def held(shape, dtype, name):
            return keep.tile(shape, dtype, name=name, align_bytes=64)

        def in_slot(shape, dtype, slot, bufs=1):
            return keep.tile(shape, dtype, name=slot, tag=slot, bufs=bufs, align_bytes=64)

        def bank(n):
            return psum.tile([P, S], F32, name="bank%d" % n, tag="bank%d" % n)

        def load_list(src, name):
            tile = keep.tile([P, S // 16], U16, name=name)
            nc.sync.dma_start(tile[:], src)
            return tile

        def load_words(words, a, slot):
            tile = in_slot([P, T], U32, slot)
            nc.sync.dma_start(out=tile[:].bitcast(I32), in_=words[a].rearrange("p t i -> p (t i)").bitcast(I32))
            return tile

        def load_rows(rows, slot):
            tile = in_slot([P, PACK, rows.shape[1]], F32, slot)
            nc.sync.dma_start(out=tile[:], in_=rows.rearrange("(p i) c -> p i c", i=PACK))
            return tile

        def move_scale_rows(queue, to_rows, from_rows):
            queue.dma_start(out=to_rows.bitcast(I32), in_=from_rows.bitcast(I32))

        def gather(window, offsets, dtype, slot):
            tile = in_slot([P, S], dtype, slot)
            nc.vector.tensor_copy(tile[:], window.indirect(offsets[:]))
            return tile

        def quantise(woven, codes, scales):
            nc.vector.quantize_mx(out=codes.bitcast(FP8X4), scales=scales, in_=woven)

        def sets_by_lines(row_sets):
            return row_sets.rearrange("p i (c e) -> p c i e", e=LINE)

        def woven_by_lines(woven):
            return woven.rearrange("p (c e i) -> p c i e", e=LINE, i=PACK)

        def as_loaded(columns):
            return columns.rearrange("p a (b m i) -> p (a b) m i", b=2, i=PACK)

        def as_dealt(places):
            return places.rearrange("p a (b i m) -> p (a b) m i", b=2, i=PACK)

        tab_sc = held([P, T], U8, "tab_sc")
        w4_sc = held([P, 2, H], U8, "w4_sc")
        tab2_sc = in_slot([P, T], U8, "scales2_then_codes")
        tab3_sc = in_slot([P, T], U8, "scales3_then_w1")
        for tile in (w4_sc, tab_sc):
            nc.vector.memset(tile[:].bitcast(I32), 0)
        seed = in_slot([P, 1], F32, "seed_then_b1")
        nc.vector.memset(seed[:], 1.0)
        phase = keep.tile([P, 1], F32, name="phase")
        nc.vector.tensor_scalar(phase[:], seed[:], -math.pi / 8, None, ALU.mult)
        for tile in (tab2_sc, tab3_sc):
            nc.vector.memset(tile[:].bitcast(I32), 0)

        idx = load_list(offs, "idx")
        tab_win = {2: load_words(tab_words, 2, "tab_win2")}
        b1_sb = in_slot([P, 2, PACK], F32, "seed_then_b1")
        nc.sync.dma_start(out=b1_sb[:], in_=b1.rearrange("(b p i) -> p b i", p=P, i=PACK))
        for q in range(QUADS):
            rows = w4_scales[:, ROWS * q : ROWS * (q + 1), :].rearrange("a r c -> r a c")
            move_scale_rows(nc.sync, w4_sc[QUAD * q : QUAD * q + ROWS, :, :], rows)
        w1_rows = {(0, 0): load_rows(w1[0:PASS, 0:PASS], "w1_then_res")}
        w4_raw = in_slot([P, 2, H], U16, "w4_then_tab")
        nc.sync.dma_start(out=w4_raw[:].bitcast(I32), in_=w4_words.rearrange("a p c -> p a c").bitcast(I32))
        for q in range(QUADS):
            move_scale_rows(
                nc.sync, tab_sc[QUAD * q : QUAD * q + 4 * ROWS, :], tab_scales[:, ROWS * q : ROWS * (q + 1), :]
            )
        tab_win[3] = load_words(tab_words, 3, "tab_win3")
        w1_rows[0, 1] = load_rows(w1[PASS : 2 * PASS, 0:PASS], "w1_rows01")
        idx2 = load_list(offs2, "idx2")
        gain_sb = keep.tile([P, 2, PACK], F32, name="gain_sb")
        nc.sync.dma_start(out=gain_sb[:], in_=gain.rearrange("(b p i) -> p b i", p=P, i=PACK))
        tab_win[0] = load_words(tab_words, 0, "tab_win0")
        for tile, scales in ((tab2_sc, tab2_scales), (tab3_sc, tab3_scales)):
            for q in range(QUADS):
                move_scale_rows(
                    nc.gpsimd,
                    tile[QUAD * q + UPPER : QUAD * q + UPPER + 2 * ROWS, :],
                    scales[:, ROWS * q : ROWS * (q + 1), :],
                )

        w1_codes, w1_scales = {}, {}

        def round_w1(engine_copy, b, a, slot):
            woven = in_slot([P, PACK * PASS], BF16, slot)
            engine_copy(
                out=woven[:].rearrange("p (i m j) -> p m j i", i=PACK, j=PACK),
                in_=w1_rows[b, a][:].rearrange("p j (m i) -> p m j i", i=PACK),
            )
            return woven

        def quantise_w1(woven, b, a):
            w1_codes[b, a] = held([P, PASS], U32, "w1_codes%d%d" % (b, a))
            w1_scales[b, a] = held([P, PASS], U8, "w1_scales%d%d" % (b, a))
            quantise(woven[:], w1_codes[b, a][:], w1_scales[b, a][:])

        v_codes = {2: gather(tab_win[2][:], idx, U32, "v_codes2")}
        w4_sc_dealt = held([P, 2, H], U8, "w4_sc_dealt")
        nc.vector.tensor_copy(out=as_dealt(w4_sc_dealt[:]), in_=as_loaded(w4_sc[:]))
        v_scales = gather(tab_sc[:], idx, U8, "v_scales")
        quantise_w1(round_w1(nc.scalar.copy, 0, 0, "w1_bf00"), 0, 0)
        w4_dealt = held([P, 2, H], U16, "w4_dealt")
        nc.scalar.copy(out=as_dealt(w4_dealt[:]), in_=as_loaded(w4_raw[:]))
        v_codes[3] = gather(tab_win[3][:], idx, U32, "v_codes3")
        v2_scales = gather(tab2_sc[:], idx2, U8, "tab_win3")
        quantise_w1(round_w1(nc.scalar.copy, 0, 1, "w1_bf01"), 0, 1)

        tab_win[1] = load_words(tab_words, 1, "w4_then_tab")
        idx3 = load_list(offs3, "idx3")
        v_scales1 = held([P, S], U8, "v_scales1")
        for q in range(QUADS):
            move_scale_rows(
                nc.sync, v_scales1[QUAD * q : QUAD * q + ROWS, :], v_scales[QUAD * q + ROWS : QUAD * q + 2 * ROWS, :]
            )
        v_planes = [v_scales[:], v_scales1[:], v_scales[2 * ROWS : P, :], v_scales[3 * ROWS : P, :]]
        w1_rows[1, 0] = load_rows(w1[0:PASS, PASS : 2 * PASS], "w1_rows10")
        w1_rows[1, 1] = load_rows(w1[PASS : 2 * PASS, PASS : 2 * PASS], "w1_rows11")
        tab2_win = [load_words(tab2_words, 0, "tab2_win0")]
        res0 = load_rows(res[0:PASS, :], "w1_then_res")
        tab2_win.append(load_words(tab2_words, 1, "tab2_win1"))
        tab3_win = [load_words(tab3_words, a, "tab3_win%d" % a) for a in range(2)]
        res1 = [load_rows(res[PASS : 2 * PASS, HALVES[jh]], "res1%d" % jh) for jh in range(2)]
        c2_sb = keep.tile([P, M_TILES], F32, name="c2_sb")
        with nc.allow_non_contiguous_dma(reason="one value of c2 for each partition and output tile"):
            nc.sync.dma_start(out=c2_sb[:], in_=c2.rearrange("(m p) -> p m", p=P))

        v_codes[0] = gather(tab_win[0][:], idx, U32, "scales2_then_codes")
        v_codes[1] = gather(tab_win[1][:], idx, U32, "tab_win0")
        v3_scales = gather(tab3_sc[:], idx3, U8, "w4_then_tab")

        y = [[bank(PACK * b + i) for i in range(PACK)] for b in range(2)]

        def first_stage_pass(b, a, start, stop):
            for i in range(PACK):
                if a < 2:
                    places = slice(PASS * b + P * i, PASS * b + P * (i + 1))
                    lhsT, lhsT_scale = w4_dealt[:, a, places].bitcast(FP4X4), w4_sc_dealt[:, a, places]
                else:
                    places = slice(P * i, P * (i + 1))
                    lhsT, lhsT_scale = w1_codes[b, a - 2][:, places].bitcast(FP8X4), w1_scales[b, a - 2][:, places]
                nc.tensor.matmul_mx(
                    out=y[b][i][:], lhsT=lhsT, lhsT_scale=lhsT_scale,
                    rhs=v_codes[a][:].bitcast(FP8X4), rhs_scale=v_planes[a],
                    start=start, stop=stop,
                )

        for a in (2, 3, 0, 1):
            first_stage_pass(0, a, start=a == 2, stop=a == 1)
        for a in (1, 0):
            first_stage_pass(1, a, start=a == 1, stop=False)

        h = [held([P, PACK, S], F32, "h%d" % b) for b in range(2)]

        def tanh_of_set(b, i):
            tile = in_slot([P, S], F32, "tanh", bufs=PACK)
            nc.scalar.activation(out=tile[:], in_=y[b][i][:], func=ACT.Tanh, bias=b1_sb[:, b, i : i + 1])
            return tile

        h_codes = [held([P, S], U32, "h_codes%d" % b) for b in range(2)]
        h_scales = [held([P, S], U8, "h_scales%d" % b) for b in range(2)]
        hr_codes0, hr_scales0 = held([P, S], U32, "hr_codes0"), held([P, S], U8, "hr_scales0")
        hr_codes1 = [held([P, HALF], U32, "hr_codes1%d" % jh) for jh in range(2)]
        hr_scales1 = [held([P, HALF], U8, "hr_scales1%d" % jh) for jh in range(2)]

        def weave_h(h_sets, slot):
            woven = in_slot([P, PACK * h_sets.shape[2]], BF16, slot)
            nc.scalar.copy(out=woven_by_lines(woven[:]), in_=sets_by_lines(h_sets))
            return woven[:]

        def weave_hr(h_sets, res_sets, slot):
            woven = in_slot([P, PACK * h_sets.shape[2]], BF16, slot)
            nc.vector.tensor_tensor(woven_by_lines(woven[:]), sets_by_lines(h_sets), sets_by_lines(res_sets), ALU.add)
            return woven[:]

        tanh0 = [tanh_of_set(0, i) for i in range(PACK)]
        woven_w1 = round_w1(nc.vector.tensor_copy, 1, 0, "scales3_then_w1")
        for i in range(PACK):
            nc.vector.tensor_scalar(h[0][:, i, :], tanh0[i][:], gain_sb[:, 0, i : i + 1], None, ALU.mult)
            if i == 0:
                quantise_w1(woven_w1, 1, 0)
        first_stage_pass(1, 2, start=False, stop=False)
        woven_h0 = weave_h(h[0][:], "woven_h0")
        quantise_w1(round_w1(nc.vector.tensor_copy, 1, 1, "scales3_then_w1"), 1, 1)
        first_stage_pass(1, 3, start=False, stop=True)

        tanh1 = []
        for step in range(PACK + 1):
            if step < PACK:
                tanh1.append(tanh_of_set(1, step))
            if step > 0:
                i = step - 1
                nc.scalar.activation(out=h[1][:, i, :], in_=tanh1[i][:], func=ACT.Copy, scale=gain_sb[:, 1, i : i + 1])
        woven_h1 = [weave_h(h[1][:, :, HALVES[jh]], "woven_h1%d" % jh) for jh in range(2)]

        v2_codes = [gather(tab2_win[0][:], idx2, U32, "scales3_then_w1")]
        quantise(woven_h0, h_codes[0][:], h_scales[0][:])
        woven_hr0 = weave_hr(h[0][:], res0[:], "woven_h0")
        v2_codes.append(gather(tab2_win[1][:], idx2, U32, "w1_then_res"))
        quantise(woven_hr0, hr_codes0[:], hr_scales0[:])
        v3_codes = [gather(tab3_win[0][:], idx3, U32, "woven_h0")]
        for jh in range(2):
            quantise(woven_h1[jh], h_codes[1][:, HALVES[jh]], h_scales[1][:, HALVES[jh]])

        e2 = [bank(m) for m in range(M_TILES)]
        for b in range(2):
            for m in range(M_TILES):
                cols = slice(P * m, P * (m + 1))
                nc.tensor.matmul_mx(
                    out=e2[m][:],
                    lhsT=v2_codes[b][:, cols].bitcast(FP8X4), lhsT_scale=v2_scales[UPPER + ROWS * b : P, cols],
                    rhs=h_codes[b][:].bitcast(FP8X4), rhs_scale=h_scales[b][:], start=b == 0, stop=b == 1,
                )

        u = [held([P, S], F32, "u%d" % m) for m in range(M_TILES)]
        for step in range(M_TILES + 2):
            if step < M_TILES:
                nc.scalar.activation(out=u[step][:], in_=e2[step][:], func=ACT.Sin, bias=phase[:], scale=0.25)
            if 1 <= step <= M_TILES:
                nc.scalar.activation(out=u[step - 1][:], in_=u[step - 1][:], func=ACT.Square)
            if step >= 2:
                nc.scalar.activation(out=u[step - 2][:], in_=u[step - 2][:], func=ACT.Square, bias=1.0, scale=-2.0)

        v3_codes.append(gather(tab3_win[1][:], idx3, U32, "woven_h11"))

        e3 = [bank(PACK + m) for m in range(M_TILES)]

        def outing_pass(b, members, codes, scales, start, stop):
            for m in range(M_TILES):
                cols = slice(P * m, P * (m + 1))
                nc.tensor.matmul_mx(
                    out=e3[m][:, members],
                    lhsT=v3_codes[b][:, cols].bitcast(FP8X4), lhsT_scale=v3_scales[UPPER + ROWS * b : P, cols],
                    rhs=codes.bitcast(FP8X4), rhs_scale=scales, start=start, stop=stop,
                )

        outing_pass(0, slice(0, S), hr_codes0[:], hr_scales0[:], start=True, stop=False)
        woven_hr1 = [
            weave_hr(h[1][:, :, HALVES[jh]], res1[jh][:], ("tab3_win1", "woven_h10")[jh]) for jh in range(2)
        ]
        for jh in range(2):
            quantise(woven_hr1[jh], hr_codes1[jh][:], hr_scales1[jh][:])
            outing_pass(1, HALVES[jh], hr_codes1[jh][:], hr_scales1[jh][:], start=False, stop=jh == 1)

        pieces = [(m, slice(0, S)) for m in range(M_TILES - 1)] + [(M_TILES - 1, members) for members in HALVES]
        for n, (m, members) in enumerate(pieces):
            score = held([P, members.stop - members.start], F32, "score%d" % n)
            nc.vector.scalar_tensor_tensor(
                out=score[:], in0=u[m][:, members], scalar=0.5, in1=e3[m][:, members], op0=ALU.subtract, op1=ALU.mult
            )
            if m < ADDS_ON_GPSIMD:
                nc.gpsimd.tensor_scalar(score[:], score[:], 2.0, c2_sb[:, m : m + 1], ALU.mult, ALU.add)
            else:
                nc.scalar.activation(out=score[:], in_=score[:], func=ACT.Identity, bias=c2_sb[:, m : m + 1], scale=2.0)
            nc.sync.dma_start(out=out[P * m : P * (m + 1), members], in_=score[:])
